import numpy as np, ml_dtypes
CORES = [2,3,42,43,82,83,122,123]
N = 8
BF = ml_dtypes.bfloat16
W, NS, TS = 4096, 128, 6
B = W // NS
def parts(rng):
    size = rng.choice(np.array([256, 256, 256, 64, 16]), (N, 8, 1, W))
    x = (rng.random((N, 8, 16, W)) * size).astype(np.int64)
    v = rng.integers(0, W, (N, 8, 16, W)); s = rng.integers(0, W, (N, 8, 16, NS)); z = rng.integers(0, 256, (N, 8, 16, NS)); w = rng.integers(0, 256, (N, 8, 16))
    h = np.where(rng.random((N, 8, 16)) < 0.75, rng.integers(0, 600, (N, 8, 16)), rng.integers(600, 1600, (N, 8, 16)))
    return x, v, s, z, w, h, rng.integers(0, 2, (N, 8, NS))
def pack(x, v, s, z, w, h, a):
    return {"reg": np.ascontiguousarray(x.reshape(N, 128, W)).astype(np.float32).astype(BF), "vw": np.ascontiguousarray((v[..., :W // 2] + W * v[..., W // 2:]).reshape(N, 128, W // 2)).astype(np.int32),
            "scan": np.ascontiguousarray(s.reshape(N, 128, NS)).astype(np.int32), "z0": np.ascontiguousarray(z.reshape(N, 128, NS)).astype(np.float32).astype(BF),
            "wt": np.ascontiguousarray(w.reshape(N, 128, 1)).astype(np.int32), "th": np.ascontiguousarray(h.reshape(N, 128, 1)).astype(np.int32), "warm": np.ascontiguousarray(a).astype(np.int32)}
def setup_inputs(rng):
    return pack(*parts(rng))
def setup_inputs_corners(rng):
    x, v, s, z, w, h, a = parts(rng); i = np.arange(NS)[None, :]; k = np.arange(16)[:, None]; d = np.arange(W)[None, :]
    for q in range(N):
        for g in range(8):
            c = (g + 3 * q) % 8
            x[q, g][:, ::7] = 0; x[q, g][:, 3::7] = 255; x[q, g][:, W - 1] = 255
            if (q + g) % 3 == 0: a[q, g] = 0
            if (q + g) % 3 == 1: a[q, g] = 1
            if c == 0: s[q, g] = 0; w[q, g] = 255
            if c == 1: s[q, g] = W - 1; h[q, g] = 4079
            if c == 2: s[q, g] = B * i + k % B; h[q, g] = 0
            if c == 3: s[q, g] = B * rng.integers(0, NS, (16, NS)); w[q, g] = 0; h[q, g] = 0; a[q, g] = rng.integers(0, 2, NS)
            if c == 4: s[q, g] = (16 * i + k + 1) % W; v[q, g] = np.where(k >= 0, (d + 1) % W, 0)
            if c == 5: v[q, g] = np.where(k >= 0, d, 0); w[q, g] = 255 * rng.integers(0, 2, 16)
            if c == 6: v[q, g] = (W - 1) * rng.integers(0, 2, (1, W)); h[q, g] = 4079 * rng.integers(0, 2, 16)
            if c == 7: s[q, g] = B * rng.integers(0, NS, (16, NS)) + B - 1; a[q, g] = rng.integers(0, 2, NS); h[q, g] = 0
            if c % 3 == 0: z[q, g] = 0
            if c % 3 == 1: z[q, g] = 255
    return pack(x, v, s, z, w, h, a)
def setup_inputs_crowd(rng):
    x, v, s, z, w, h, a = parts(rng); h = rng.integers(0, 1000, (N, 8, 16))
    for q in range(N):
        for g in range(8):
            pl = rng.permutation(W)[:4]; x[q, g][:, pl[:3]] = rng.integers(200, 256, (16, 3)); x[q, g][:, pl[3]] = 0
            s[q, g] = rng.choice(pl[:1 + 2 * (g % 2)], (16, NS)); a[q, g] = 1
            if g % 4 == 1: w[q, g] = 0
            if g % 4 == 2: w[q, g] = 255
            o = int(rng.integers(0, NS)) if g < 7 else NS - 1
            if q % 4 == 3:
                a[q, g] = 0
                if g == 7: a[q, g, o] = 1
            elif (q % 4 == 1 and g == 7) or (q % 4 == 2 and g % 2 == 1):
                way = (g // 2 + q) % 3
                if way == 0: a[q, g, o] = 0
                else: s[q, g, :, o] = pl[3]
                if way == 2: s[q, g, int(rng.integers(0, 16)), o] = pl[0]
    return pack(x, v, s, z, w, h, a)
def setup_inputs_ends(rng):
    x = np.where(rng.random((N, 8, 1, W)) < 0.5, 255 * rng.integers(0, 2, (N, 8, 1, W)), 255 * rng.integers(0, 2, (N, 8, 16, W)))
    x[..., 0] = 0; x[..., W - 1] = 255; x[:, 1, :, 0] = 255; x[:, 1, :, W - 1] = 0
    e = (W - 1) * rng.integers(0, 2, (N, 8, 16, W // 2)); c = rng.random(e.shape) < 0.7
    v = np.concatenate([np.where(c, e, rng.integers(0, W, e.shape)), np.where(c, e, rng.integers(0, W, e.shape))], axis=3)
    s = np.where(rng.random((N, 8, 16, NS)) < 0.72, (W - 1) * rng.integers(0, 2, (N, 8, 16, NS)), rng.integers(0, W, (N, 8, 16, NS)))
    z = np.where(rng.random((N, 8, 1, NS)) < 0.5, 255 * rng.integers(0, 2, (N, 8, 1, NS)), 255 * rng.integers(0, 2, (N, 8, 16, NS)))
    w = 255 * rng.integers(0, 2, (N, 8, 16)); w[:, 2] = 255; w[:, 6] = 255
    w[:, 3] = 0; w[:, 3, 15] = 255; w[:, 3, 0] = 2; w[:, 7] = w[:, 3]; w[0, 7] = 255
    h = 4079 * rng.integers(0, 2, (N, 8, 16)); h[..., 0] = 4079; h[..., 8] = 0; h[..., 15] = 0
    a = (rng.random((N, 8, NS)) < 0.6).astype(np.int64); i = np.arange(NS); last = i[i % 8 == 7]; one = i[i % 8 == 6]; two = i[i % 8 == 1]; three = i[i % 8 == 5]; late = 5 * B - 1
    for q in range(N):
        b = (N - 1 - q) % 2 == 0
        v[q, :, :, W - 1] = W - 1 if b else 0; v[q, :, :, W // 2 - 1] = W - 1 if b else 0
        s[q][:, :, last] = W - 1; z[q][:, :, last] = 0 if b else 255; a[q][:, last] = 1
        if b:
            both = np.concatenate([one, two]); s[q][:, :, both] = 0; z[q][:, :, both] = 255; a[q][:, both] = 1
            s[q][:, 15, one] = W - 1; s[q][:, 8, two] = W - 1
            for g in (3, 7):
                x[q, g][:, late] = 0; s[q, g][:, 4] = W - 1; z[q, g][:, 4] = 0; a[q, g, 4] = 1
                s[q, g][:, three] = 0; s[q, g][15, three] = W - 1; s[q, g][8, three] = late; z[q, g][:, three] = 0; a[q, g, three] = 1
    s[0, :, 3] = W - 1; s[0, :, 15] = W - 1; s[0, 1, 3] = 0; s[0, 1, 15] = 0; a[0] = 1; a[0, 0, 0] = 0
    return pack(x, v, s, z, w, h, a)
def setup_inputs_spread(rng):
    x, v, s, z, w, h, a = parts(rng)
    x = (np.exp2(8 * rng.random((N, 8, 1, W))) * rng.random((N, 8, 16, W))).astype(np.int64)
    z = (np.exp2(8 * rng.random((N, 8, 1, NS))) * rng.random((N, 8, 16, NS))).astype(np.int64)
    w = np.minimum(np.exp2(8 * rng.random((N, 8, 16))).astype(np.int64), 255); h = np.minimum(np.exp2(12 * rng.random((N, 8, 16))).astype(np.int64) - 1, 4079)
    p = rng.choice(np.array([0.5, 1.0, 2.0, 3.0]), (N, 8, 1, 1))
    s = np.minimum((W * rng.random((N, 8, 16, NS)) ** p).astype(np.int64), W - 1); v = np.minimum((W * rng.random((N, 8, 16, W)) ** p).astype(np.int64), W - 1)
    a = (rng.random((N, 8, NS)) < rng.choice(np.array([0.1, 0.5, 0.9]), (N, 8, 1))).astype(np.int64)
    return pack(x, v, s, z, w, h, a)
def setup_inputs_ties(rng):
    x, v, s, z, w, h, a = parts(rng); lane = np.arange(16)[:, None]
    for q in range(N):
        for g in range(8):
            if g % 2 == 0:
                c = (0, 16, 1000, 4079)[(g // 2 + q) % 4]
                m = np.minimum(np.maximum(c + rng.integers(-1, 2, W), 0), 4080)
                x[q, g] = m // 16 + ((lane + rng.integers(0, 16, W)) % 16 < m % 16); h[q, g] = c
                z[q, g] = z[q, g] * rng.integers(0, 2, (1, NS)); a[q, g] = rng.random(NS) < 0.8
            else:
                x[q, g] = rng.integers(0, 16, (16, W)); x[q, g][:, W // 2:] = x[q, g][:, :W // 2]
                s[q, g, 1::2] = (s[q, g, 0::2] + W // 2) % W; h[q, g] = rng.integers(10, 70, 16); z[q, g] = rng.integers(0, 16, (16, NS))
                x[q, g][:, 5] = 255; x[q, g, (g + q) % 16, 5] = 254; x[q, g][:, W - 1] = 255
                s[q, g][:, NS - 2:] = 5; s[q, g, 15, NS - 2:] = W - 1; z[q, g][:, NS - 2:] = 0; a[q, g, NS - 2:] = 1
                if g % 4 == 3:
                    x[q, g][:, W - 3] = 0; x[q, g][:, W // 2 - 3] = 0; w[q, g, 0] = 1; w[q, g, 1] = 16
                    s[q, g][:, 4:6] = W - 3; z[q, g][:, 4:6] = 0; z[q, g, 0, 4:6] = 11; z[q, g, 1, 4:6] = W // 16 - 2; a[q, g, 4:6] = 1
    return pack(x, v, s, z, w, h, a)
def check_inputs(d):
    bad = []
    for k, lo, hi in (("reg", 0, 255), ("vw", 0, W * W - 1), ("scan", 0, W - 1), ("z0", 0, 255), ("wt", 0, 255), ("th", 0, 4079), ("warm", 0, 1)):
        a = np.asarray(d[k]).astype(np.float64)
        if not (np.min(a) >= lo and np.max(a) <= hi): bad.append("range of " + k)
        elif np.any(a != np.floor(a)): bad.append("whole numbers in " + k)
    return bad
def pick(x, ix):
    return np.take_along_axis(x, ix.reshape(N, 8, 1, 16 * NS), 3).reshape(N, 8, 16, 16, NS)
def reference(reg, vw, scan, z0, wt, th, warm):
    X = reg.astype(np.float32).astype(np.int32).reshape(N, 8, 16, W); pk = vw.astype(np.int64).reshape(N, 8, 16, W // 2)
    V = np.concatenate([pk % W, pk // W], axis=3)
    S = scan.astype(np.int64).reshape(N, 8, 16, NS); z = z0.astype(np.float32).astype(np.int32).reshape(N, 8, 16, NS)
    wl = wt.astype(np.int64).reshape(N, 8, 16, 1); theta = th.astype(np.int64).reshape(N, 8, 16, 1); new = warm == 0
    last = np.zeros((N, 8, 16, 16, NS), np.int32); m = np.zeros((N, 8, 16, NS), np.int64); A = np.zeros((N, 1, 1, 1), np.int64)
    row37 = 37 * np.arange(16).reshape(1, 1, 16, 1); sc = np.arange(NS)
    for t in range(TS):
        C = pick(X, S)
        moved = (np.add.reduce(np.abs(C - last), axis=2) > theta + A % 32) & ~new[:, :, None, :]
        m = m + moved; some = np.any(moved, axis=2)
        clean = ~new & ~some; borrow = some & (np.add.reduce(m, axis=2) >= 2); has = clean | borrow
        key = 4096 * m + np.add.reduce(np.abs(C - z[:, :, :, None, :]), axis=2)
        donor = np.argmax(key, axis=2)
        dr = np.take_along_axis(S, donor[:, :, None, :], 2)
        F = np.where(borrow[:, :, None, :], np.take_along_axis(V, dr, 3), S)
        D = pick(X, F); y = (np.max(D, axis=3) + np.min(D, axis=3)) >> 1
        z = np.where(has[:, :, None, :], np.abs(y - z), z)
        u = np.add.reduce(wl * z, axis=2, keepdims=True) % W
        place = B * sc + u[:, :, 0, :] % B
        X = X.copy(); V = V.copy()
        for r in range(N):
            for odd in range(2):
                q = (r + odd * (1 + t % 3)) % N
                gi, si = np.nonzero(has[r] & (sc % 2 == odd)); pl = place[r][gi, si]
                X[q][gi, :, pl] = y[r][gi, :, si]
                if t < TS - 1: V[q][gi, :, pl] = F[r][gi, :, si]
        S = np.where(has[:, :, None, :], (((F * u) >> 5) + F + row37 + A) % W, S)
        m = np.where(has[:, :, None, :], 0, m); new = has; last = C
        A = np.add.reduce(borrow.astype(np.int64).reshape(N, 8 * NS), axis=1).reshape(N, 1, 1, 1)
    return {"yx": X.reshape(N, 128, W).astype(np.float32).astype(BF), "ys": S.reshape(N, 128, NS).astype(np.float32), "yz": z.reshape(N, 128, NS).astype(np.float32).astype(BF)}

from concourse.mybir import AluOpType as A, ActivationFunctionType as AF, AxisListType as AX

BF, F32, I32, U16 = "bfloat16", "float32", "int32", "uint16"
NSTEP = 6
ZC = 4096
SB = 4104
VW = 4232
TR = 8192
WIN = 12288
SC = 2.0 ** -17
CY = 0.83e-3 * 1.25
WAKE = 0.1
ENG = 8

SCRATCH = {
    "X": ("sbuf", [128, WIN], BF), "Q": ("sbuf", [128, WIN], BF), "V": ("sbuf", [128, WIN], I32),
    "vwb": ("sbuf", [128, 2048], I32), "zx": ("sbuf", [128, 2048], BF), "cols": ("sbuf", [128, 32], F32), "GI": ("sbuf", [128, 128], BF), "wmf": ("sbuf", [128, 128], BF),
    "msg": ("sbuf", [128, NSTEP * 72], BF), "rxy": ("sbuf", [128, NSTEP * 72], BF), "rxf": ("sbuf", [128, NSTEP * 64], U16),
    "fs": ("sbuf", [128, 48], F32), "fi": ("sbuf", [128, 16], I32), "Te": ("sbuf", [128, 160], F32), "To": ("sbuf", [128, 160], F32),
}
for _w, _d, _names in (
        (1, I32, "wb thb"), (8, I32, "J8 JJ"), (8, F32, "BASE JS JN JZ TB XS HAS HX"), (8, BF, "BO"), (8, U16, "ov oz L0 L1"),
        (64, I32, "KC1"), (64, F32, "THB THC"), (64, BF, "yE0 yE1"),
        (128, I32, "scb wmb si sj Ri vi ym yi"), (128, BF, "dz zb Z0 Z1 WB ONE WpR WpH WpY WpM WpX qm qx Qn QR zo"), (128, U16, "zl S16 F0 F1 F2 F3 F4 F5"),
        (128, F32, "ky dd GG DR um us OF blk ID UP DN E0 E1 Sa Sb MQ Kc RS1 MV NS WX so"), (144, I32, "PI NI N15 PQ PG NQ NG ti tj"), (144, F32, "tf tg Sf0 Sf1"),
        (144, BF, "W1 WT2 WTm WQ WQ0"), (1024, BF, "T0 T1 C0 C1 D0 D1 mx mn RSM RSN")):
    for _n in _names.split():
        SCRATCH[_n] = ("sbuf", [128, _w], _d)
PSUM = ("Ro", "Re", "Sx", "Uo", "Ue", "PQs", "P7", "VB")
for _n in PSUM:
    SCRATCH[_n] = ("psum", [128, 512], F32)
LOADS = ["scb", "zb", "wb", "thb", "wmb", "vwb", "X0", "X1", "X2", "X3"]
SEMAPHORES = ["sv", "ss", "sp", "sg", "ls", "dyx", "dys", "dyz"] + ["d" + n for n in LOADS] + ["ry%d" % t for t in range(NSTEP)] + ["rf%d" % t for t in range(NSTEP - 1)]


def rank_program(g, core, T, topo):
    rank = T.rank_of(core)
    if rank is None:
        return
    queues = {"v": g.vector, "s": g.scalar, "p": g.tensor, "g": g, "y": g.sync}
    own = {"v": "sv", "s": "ss", "p": "sp", "g": "sg"}
    total = {}
    know = {q: {} for q in queues}
    ops = []
    hist = {}

    def h(name, lo=0, hi=None, step=1, rows=None):
        return (name, lo, T[name].shape[1] if hi is None else hi, step, rows)

    def ind(win, off):
        return ("ind", win, off)

    def ap(x):
        if x[0] == "ind":
            return ap(x[1]).indirect(ap(x[2]))
        t = T[x[0]]
        if x[4]:
            return t[0:x[4], x[1]:x[2]]
        return t[:, x[1]:x[2]] if x[3] == 1 else t[:, x[1]:x[2]:x[3]]

    def regions(x):
        return [x[1], x[2]] if x[0] == "ind" else [x]

    def wait(q, tok, clock):
        if know[q].get(tok[0], 0) >= tok[1]:
            return
        queues[q].wait_ge(T.sem[tok[0]], tok[1])
        for s, v in clock.items():
            if know[q].get(s, 0) < v:
                know[q][s] = v

    def need(q, reads, writes):
        todo = []
        for wr, group in ((False, reads), (True, writes)):
            for x in group:
                for e in hist.get(x[0], []):
                    if e[3] == q and q == "p":
                        continue
                    ps = x[0] in PSUM and e[3] != q
                    if not ps and (e[0] >= x[2] or e[1] <= x[1]):
                        continue
                    if (e[2] or wr or ps) and (e[4], e[5]) not in todo:
                        todo.append((e[4], e[5]))
        todo.sort(key=lambda c: -len(c[1]))
        for tok, clock in todo:
            wait(q, tok, clock)

    def note(q, tok, reads, writes, tag=None):
        clock = dict(know[q])
        clock[tok[0]] = tok[1]
        tag = tag or q
        for wr, group in ((True, writes), (False, reads)):
            for x in group:
                lo, hi = x[1], x[2]
                lst = hist.setdefault(x[0], [])
                if wr:
                    lst[:] = [e for e in lst if not (e[0] >= lo and e[1] <= hi)]
                else:
                    lst[:] = [e for e in lst if not (not e[2] and e[3] == tag and e[0] >= lo and e[1] <= hi and tag in own)]
                lst.append((lo, hi, wr, tag, tok, clock))

    def bump(sem, n):
        total[sem] = total.get(sem, 0) + n
        return (sem, total[sem])

    def schedule():
        n = len(ops)
        pred, seen = [[] for _ in ops], {}
        for i, (q, _e, reads, writes, us, lat, tag) in enumerate(ops):
            for wr, group in ((False, reads), (True, writes)):
                for x in group:
                    for e in seen.get(x[0], []):
                        ps = x[0] in PSUM and e[3] != tag
                        if not ps and (e[0] >= x[2] or e[1] <= x[1]):
                            continue
                        if e[2] or wr or ps:
                            pred[i].append(e[4])
            for wr, group in ((True, writes), (False, reads)):
                for x in group:
                    lst = seen.setdefault(x[0], [])
                    if wr:
                        lst[:] = [e for e in lst if not (e[0] >= x[1] and e[1] <= x[2])]
                    lst.append((x[1], x[2], wr, tag, i))
        succ, left = [[] for _ in ops], [0] * n
        for i in range(n):
            pred[i] = sorted(set(pred[i]))
            left[i] = len(pred[i])
            for j in pred[i]:
                succ[j].append(i)
        rest = [0.0] * n
        for i in range(n - 1, -1, -1):
            rest[i] = ops[i][4] + ops[i][5] + max([rest[j] + WAKE for j in succ[i]] + [0.0])
        ready, free = [0.0] * n, {}
        cand = [i for i in range(n) if not left[i]]
        while cand:
            st, _r, i = min([(max(ready[i], free.get(ops[i][0], 0.0)), -rest[i], i) for i in cand])
            cand.remove(i)
            free[ops[i][0]] = st + ops[i][4]
            for j in succ[i]:
                w = 0.0 if ops[i][0] == ops[j][0] == "p" else WAKE
                ready[j] = max(ready[j], st + ops[i][4] + ops[i][5] + w)
                left[j] -= 1
                if not left[j]:
                    cand.append(j)
            ops[i][1]()

    def elems(x):
        return 16 * (x[2][2] - x[2][1]) if x[0] == "ind" else -(-(x[2] - x[1]) // x[3])

    def vtime(o, ins, cyc):
        n = elems(o)
        if o[0] == "ind":
            return 0.05 + 3.8 * n * CY
        if [x for x in ins if x[0] == "ind"]:
            return 0.05 + 1.56 * n * CY
        return max(64.0, cyc * n) * CY

    def rate(*xs):
        return 1.0 if [x for x in xs if SCRATCH[x[1][0] if x[0] == "ind" else x[0]][2] in (F32, I32)] else 0.5

    def run(q, call, out, ins, us):
        reads = [r for x in ins for r in regions(x)] + regions(out)[1:]
        writes = regions(out)[:1]

        def emit():
            need(q, reads, writes)
            call().then_inc(T.sem[own[q]], 1)
            note(q, bump(own[q], 1), reads, writes)
        ops.append((q, emit, reads, writes, us, 0.0, q))

    V, S = g.vector, g.scalar

    def tt(o, x, y, op):
        run("v", lambda: V.tensor_tensor(ap(o), ap(x), ap(y), op), o, [x, y], vtime(o, [x, y], 1.0 if x[0] in PSUM or y[0] in PSUM else 2.0))

    def ts(o, x, s1, op0, s2=None, op1=None):
        ins = [x] + [s for s in (s1, s2) if isinstance(s, tuple)]
        c1 = ap(s1) if isinstance(s1, tuple) else s1
        if op1 is None:
            run("v", lambda: V.tensor_scalar(ap(o), ap(x), c1, None, op0), o, ins, vtime(o, [x], rate(o, x)))
        else:
            run("v", lambda: V.tensor_scalar(ap(o), ap(x), c1, s2, op0, op1), o, ins, vtime(o, [x], rate(o, x)))

    def cp(o, x):
        run("v", lambda: V.tensor_copy(ap(o), ap(x)), o, [x], vtime(o, [x], rate(o, x)))

    def fill(o, c):
        run("v", lambda: V.memset(ap(o), c), o, [], vtime(o, [], 1.0))

    def scan(o, d0, d1, init, op0, op1):
        run("v", lambda: V.tensor_tensor_scan(ap(o), ap(d0), ap(d1), init, op0, op1), o, [d0, d1], vtime(o, [], rate(o, d0, d1)))

    def turn(o, x):
        run("v", lambda: V.transpose(ap(o), ap(x)), o, [x], vtime(o, [], 1.0))

    def act(o, x, f, bias=0.0):
        us = 0.065 + 1.56 * elems(o) * CY if x[0] == "ind" else max(64, elems(o)) * CY
        if f == AF.Copy:
            run("s", lambda: S.activation(ap(o), ap(x), f), o, [x], us)
        else:
            run("s", lambda: S.activation(ap(o), ap(x), f, bias=bias), o, [x], us)

    def times(o, x, s):
        c = ap(s) if isinstance(s, tuple) else s
        run("s", lambda: S.activation(ap(o), ap(x), AF.Identity, scale=c), o, [x] + ([s] if isinstance(s, tuple) else []), max(64, elems(o)) * CY)

    def iota(o, pattern, base, cm, small=False):
        run("g", lambda: g.iota(ap(o), pattern, base, cm, allow_small_or_imprecise_dtypes=small), o, [], 0.13 + 2 * elems(o) * CY)

    def diag(o, base):
        run("g", lambda: g.affine_select(ap(o), ap(h("OF")), [[1, 128]], A.is_equal, 0.0, base, -1), o, [h("OF")], 0.17 + 2 * elems(o) * CY)

    def mms(out, pairs, start=True, stop=True):
        reads = [x for p in pairs for x in p]
        us = len(pairs) * max(64, elems(out)) * CY * (4 if SCRATCH[pairs[0][0][0]][2] == F32 else 1)

        def emit():
            need("p", reads, [out])
            for n, (l, r) in enumerate(pairs):
                i = g.tensor.matmul(ap(out), ap(l), ap(r), start and n == 0, stop and n == len(pairs) - 1)
            i.then_inc(T.sem["sp"], 1)
            note("p", bump("sp", 1), reads, [out])
        ops.append(("p", emit, reads, [out], us, 0.0, "p"))

    def dma(q, sem, out, in_, ohandle=None, ihandle=None):
        reads, writes = ([ihandle] if ihandle else []), ([ohandle] if ohandle else [])

        def emit():
            need(q, reads, writes)
            queues[q].dma_start(out, in_).then_inc(T.sem[sem], 16)
            note(q, bump(sem, 16), reads, writes, q + "dma")
        ops.append((q, emit, reads, writes, 0.06, 3.0, q + "dma"))

    def send(out, in_, remote, dst):
        rid, pid, _se = topo.addr(dst)
        eng = topo.engines(core, dst)[:ENG]
        m = 0
        for e in eng:
            m |= 1 << e

        def emit():
            need("g", [in_], [])
            g.remote_dma(ap(out), ap(in_), T.sem[remote], T.sem["ls"], pid, rid, m)
            bump("ls", len(eng))
        ops.append(("g", emit, [in_], [("@" + remote, 0, 1, 1)], 0.8, 0.0, "g"))

    def recv(out, sem, n):
        def emit():
            hist.setdefault(out[0], []).append((out[1], out[2], True, "remote", bump(sem, n), {sem: n}))
        ops.append(("remote" + sem, emit, [("@" + sem, 0, 1, 1)], [out], 2.5, 0.0, "remote"))

    for b, t in (("scb", T.scan), ("zb", T.z0), ("thb", T.th), ("wb", T.wt)):
        dma("y", "d" + b, ap(h(b)), t[:, :], h(b))
    for n in range(4):
        dma("s", "dX%d" % n, ap(h("X", 1024 * n, 1024 * n + 1024)), T.reg[:, 1024 * n:1024 * n + 1024], h("X", 1024 * n, 1024 * n + 1024))
    dma("y", "dwmb", T["wmb"][0:8, :], T.warm[:, :], h("wmb"))
    dma("y", "dvwb", ap(h("vwb")), T.vw[:, :], h("vwb"))

    m128 = lambda b: h(b, 0, 128)
    col = lambda c: h("cols", c, c + 1)
    QC, H0, H1, LQ, L0C, K37, AK0, AK1, CA, WC, THN, C64, A1, G0, G1, LQ1 = range(16)
    half = lambda hh: (64 * hh, 64 * hh + 64)
    four = lambda hh: (4 * hh, 4 * hh + 4)
    fill(h("OF"), 1.0)
    iota(h("PI"), [[0, 144]], 0, 1)
    iota(h("NI"), [[1, 144]], 0, 0)
    diag(h("ID"), 0)
    diag(h("UP"), -16)
    diag(h("DN"), 16)
    iota(h("N15"), [[1, 144]], -15, 0)
    iota(h("KC1"), [[16384, 4], [0, 16]], 0, 0)
    iota(h("J8"), [[32, 2], [1024, 4]], 0, 0)
    iota(h("JJ"), [[16, 8]], 0, 0)
    iota(h("RSM"), [[0, 64], [256, 16]], 0, 0, True)
    iota(h("RSN"), [[0, 64], [-255, 16]], 255, 0, True)
    iota(h("X", ZC, ZC + 16), [[0, 16]], 0, 0, True)
    iota(h("X", TR, WIN), [[0, WIN - TR]], 0, 0, True)
    ts(h("PQ"), h("PI"), 15, A.bitwise_and)
    ts(h("PG"), h("PI"), 112, A.bitwise_and)
    ts(h("NG"), h("NI"), 112, A.bitwise_and)
    ts(h("fi", 0, 1), h("PI", 0, 1), 4, A.logical_shift_right, 1, A.bitwise_and)
    ts(col(H1), h("fi", 0, 1), SC, A.mult)
    ts(col(H0), col(H1), -1.0, A.mult, SC, A.add)
    ts(col(G1), h("fi", 0, 1), 1.0, A.mult)
    ts(col(G0), col(G1), -1.0, A.mult, 1.0, A.add)
    ts(h("ti"), h("PI"), 1, A.logical_shift_right, 7, A.bitwise_and)
    tt(h("ti"), h("ti"), h("PG"), A.add)
    tt(h("WpR"), m128("ti"), m128("NI"), A.is_equal)
    tt(h("tj"), h("NG"), h("PQ"), A.add)
    cp(h("zl"), m128("tj"))
    fill(h("Te"), 0.0)
    fill(h("To"), 0.0)
    for nm, src, cc in (("E0", "ID", H0), ("E1", "ID", H1), ("Sa", "UP", H0), ("Sb", "DN", H1)):
        times(h(nm), h(src), col(cc))
    act(h("Z0", 64, 128), h("zb", 1, 128, 2), AF.Copy)
    act(h("Z0", 0, 64), h("zb", 0, 128, 2), AF.Copy)
    cp(h("V", SB, SB + 64), h("scb", 0, 128, 2))
    cp(h("V", SB + 64, SB + 128), h("scb", 1, 128, 2))

    def relocate_vector():
        ts(m128("Sf0"), h("V", SB, SB + 128), col(G0), A.mult)
        ts(m128("Sf1"), h("V", SB, SB + 128), col(G1), A.mult)
        turn(h("Te", 16, 144), m128("Sf0"))
        turn(h("To", 16, 144), m128("Sf1"))

    def relocate_tensor():
        mms(h("Sx", 0, 128), [(h("E0"), h("Te", 16, 144)), (h("Sa"), h("To", 32, 160)), (h("E1"), h("To", 16, 144)), (h("Sb"), h("Te", 0, 128))])

    def relocate_list():
        ts(h("S16"), h("Sx", 0, 128), 1.0 / SC, A.mult)

    def refresh_zx(z, hh):
        act(h("zx", 1024 * hh, 1024 * hh + 1024), ind(h(z), h("zl", *half(hh))), AF.Copy)

    banks = ["Uo", "Ue", "PQs", "P7"]

    refresh_zx("Z0", 1)
    relocate_vector()
    relocate_tensor()
    for n in range(8):
        b = h(banks[n % 4], 0, 512)
        mms(b, [(h("WpR"), h("X", 512 * n, 512 * n + 512))])
        act(h("Q", 512 * n, 512 * n + 512), b, AF.Identity, -255.0)
    tt(h("W1"), h("PG"), h("N15"), A.is_equal)
    ts(col(LQ1), h("PQ", 0, 1), 8.0, A.is_lt)
    ts(col(L0C), col(LQ1), 4096.0, A.mult)
    ts(col(LQ), col(LQ1), -4097.0, A.mult, 4096.0, A.add)
    relocate_list()
    times(h("WTm"), h("W1"), -1.0)
    times(h("WT2"), h("W1"), 2.0)
    times(h("WQ"), h("W1"), col(LQ))
    times(h("WQ0"), h("W1"), col(L0C))
    ts(h("NQ"), h("NI"), 15, A.bitwise_and)
    tt(h("blk"), m128("PG"), m128("NG"), A.is_equal)
    tt(h("MQ"), m128("PQ"), m128("NQ"), A.is_equal)
    ts(col(THN), h("thb"), 1.0, A.mult)
    times(m128("tf"), h("MQ"), col(THN))
    mms(h("Ro", 0, 64), [(h("blk"), h("tf", 0, 64))])
    ts(h("THB"), h("Ro", 0, 64), -4096.0, A.mult, 4096.0 * 2039 - 2040, A.add)
    ts(h("THC"), h("THB"), 4096.0 * 2040, A.add)
    ts(h("tj", 0, 128, 1, 8), h("PI", 0, 128, 1, 8), 16.0, A.mult)
    tt(h("GI", 0, 128, 1, 8), h("NG", 0, 128, 1, 8), h("tj", 0, 128, 1, 8), A.is_equal)
    cp(h("wmf", 0, 128, 1, 8), h("wmb", 0, 128, 1, 8))
    mms(h("VB", 0, 128), [(h("GI", 0, 128, 1, 8), h("wmf", 0, 128, 1, 8))])

    def start_z(hh):
        mms(h("Ro" if hh else "Re", 0, 64), [(h("WTm", 15 - q, 143 - q), h("zx", 1024 * hh + q, 1024 * hh + 1024, 16)) for q in range(16)], True, False)

    def start_t(hh):
        mms(h("Ro" if hh else "Re", 0, 64), [(h("ID"), h("THC"))], False, False)

    def constants():
        ts(h("RS1"), m128("NQ"), 1.0, A.min)
        ts(m128("tg"), m128("NQ"), -0.0625, A.mult, 0.9375, A.add)
        for hh in (0, 1):
            tt(h("Kc", *half(hh)), h("tg", 0, 64), h("KC1"), A.add)
        tt(h("tf", 0, 64), h("VB", 0, 128, 2), h("MQ", 0, 64), A.mult)
        tt(h("tf", 64, 128), h("VB", 1, 128, 2), h("MQ", 0, 64), A.mult)
        ts(col(QC), h("PQ", 0, 1), 1.0, A.mult)
        ts(h("JS"), h("JJ"), col(QC), A.add, float(SB), A.add)
        cp(h("VB", 384, 512), h("Kc"))
        ts(h("JS"), h("JS"), SC, A.mult)
        scan(h("WX"), h("RS1"), m128("tf"), 0.0, A.mult, A.add)
        fill(h("V", ZC, ZC + 8), ZC)
        ts(h("HX"), h("WX", 15, 128, 16), -1.0, A.mult, 1.0, A.add)
        ts(h("TB"), h("HX"), 1.0e6, A.mult, 8192.0, A.add)
        tt(h("JN"), h("JS"), h("HX"), A.subtract)
        fill(h("WX"), 0.0)

    def constants2():
        ts(col(K37), col(QC), 37.0, A.mult)
        ts(col(C64), col(QC), 64.0, A.mult)
        ts(h("ti"), h("ti"), 8.0, A.add)
        ts(col(WC), h("wb"), 1.0, A.mult)
        cp(col(AK0), col(K37))
        ts(h("BASE"), h("J8"), col(C64), A.add)
        tt(h("WpH"), m128("ti"), m128("NI"), A.is_equal)
        times(h("WB"), h("blk"), col(WC))
        ts(h("JZ"), h("JJ"), col(QC), A.add, 64.0, A.mult)
        tt(h("WpY"), h("WpR"), h("WpH"), A.subtract)
        times(h("WpM"), h("WpH"), 2.0)
        times(h("WpX"), h("WpH"), -1.0)
        fill(h("ONE"), 1.0)

    def gathers(hh):
        lst = h("S16", *half(hh))
        tt(h("T%d" % hh), ind(h("X", 0, 4096), lst), h("zx", 1024 * hh, 1024 * hh + 1024), A.max)
        act(h("C%d" % hh), ind(h("Q", 0, 4096), lst), AF.Copy)

    def sums(t, hh):
        r = h("Ro" if hh else "Re", 0, 64)
        part = lambda w, b: [(h(w, 15 - q, 143 - q), h("%s%d" % (b, hh), q, 1024, 16)) for q in range(16)]
        mms(r, part("WT2", "T"), False, False)
        mms(r, part("WQ", "C"), False, t > 0)
        if t == 0:
            mms(r, part("WQ0", "C"), False, True)

    def keys(t, hh):
        c, f = half(hh), four(hh)
        r = h("Ro" if hh else "Re", 0, 64)
        vb = lambda n: h("VB", 128 * n + c[0], 128 * n + c[1])
        ns = h("NS", c[0] + 15, c[1], 16)
        x = lambda n: h("fs", 4 * n + 16 * hh, 4 * n + 4 + 16 * hh)
        ts(h("MV", *c), r, 0.0, A.is_ge, 4096.0, A.mult)
        cp(h("Ri", *c), r)
        tt(vb(0), h("MV", *c), vb(3), A.add)
        ts(h("vi", *c), h("Ri", *c), 4095, A.bitwise_and)
        scan(h("NS", *c), h("RS1", 0, 64), h("MV", *c), 0.0, A.mult, A.add)
        tt(h("ky", *c), vb(0), h("vi", *c), A.add)
        tt(x(0), h("TB", *f), ns, A.subtract)
        scan(vb(1), h("ky", *c), h("ky", *c), -1.0, A.max, A.max)
        tt(x(1), h("JN", *f), ns, A.subtract)
        tt(h("dd", *c), vb(1), h("ky", *c), A.subtract)
        ts(x(0), x(0), ZC * SC, A.min)
        tt(h("GG", *c), h("Sx", *c), h("dd", *c), A.subtract)
        tt(x(2), x(0), x(1), A.max)
        scan(h("DR", *c), h("dd", *c), h("GG", *c), 0.0, A.min, A.max)
        tt(h("XS", *f), h("DR", c[0] + 15, c[1], 16), x(2), A.max)
        ts(h("ov", *f), h("XS", *f), 1.0 / SC, A.mult)
        cp(h("F%d" % t, *c), ind(h("V", 0, VW), h("ov", *f)))

    def dgather(t, hh, n):
        a = 32 * n
        act(h("D%d" % hh, 16 * a, 16 * a + 512), ind(h("X", 0, 4112), h("F%d" % t, 64 * hh + a, 64 * hh + a + 32)), AF.Copy)

    def extremes(hh):
        for a, b in ((0, 512), (512, 1024)):
            scan(h("mx", a, b), h("RSM", a, b), h("D%d" % hh, a, b), 0.0, A.min, A.max)
            scan(h("mn", a, b), h("RSN", a, b), h("D%d" % hh, a, b), 255.0, A.max, A.min)

    def y_of(t, hh):
        c = half(hh)
        tt(h("ym", *c), h("mx", 15, 1024, 16), h("mn", 15, 1024, 16), A.add)
        ts(h("yi", *c), h("ym", *c), 1, A.arith_shift_right)
        tt(h("dz", *c), h("yi", *c), h("Z%d" % (t % 2), *c), A.subtract)
        zn = h("Z%d" % ((t + 1) % 2), *c)
        act(zn, h("dz", *c), AF.Abs)
        cp(h("msg", 72 * t, 72 * t + 64) if hh else h("yE%d" % (t % 2)), h("yi", *c))
        mms(h("Uo" if hh else "Ue", 0, 64), [(h("WB"), zn)])

    def place(t, hh):
        c, f = half(hh), four(hh)
        fi = lambda n: h("fi", 4 * n, 4 * n + 4)
        tt(h("um", *c), h("Uo" if hh else "Ue", 0, 64), h("MQ", 0, 64), A.mult)
        scan(h("us", *c), h("RS1", 0, 64), h("um", *c), 0.0, A.mult, A.add)
        cp(fi(2 * hh), h("us", c[0] + 15, c[1], 16))
        ts(fi(2 * hh + 1), fi(2 * hh), 31, A.bitwise_and)
        if hh:
            tt(h("msg", 72 * t + 64, 72 * t + 68), fi(3), h("HX", *f), A.add)
        else:
            tt(h("fs", 36, 40), fi(1), h("fs", 32, 36), A.add)
            cp(h("L%d" % (t % 2), *f), h("fs", 36, 40))

    def write_half(t, hh, y):
        c = half(hh)
        lst = h("L%d" % (t % 2), *four(hh))
        win = h("X", 0, WIN)
        if t == NSTEP - 1:
            cp(ind(win, lst), y)
            return
        act(h("qx", *c), ind(win, lst), AF.Copy)
        tt(h("qm", *c), ind(win, lst), y, A.max)
        pq = h("PQs", *c)
        mms(pq, [(h("WpY"), y), (h("WpX"), h("qx", *c)), (h("WpM"), h("qm", *c))])
        cp(ind(win, lst), y)
        act(h("Qn", *c), pq, AF.Identity, -255.0)
        cp(ind(h("Q", 0, WIN), lst), h("Qn", *c))

    x8 = lambda n: h("tg", 8 * n, 8 * n + 8)

    def books1(t):
        ts(h("HX"), h("XS"), ZC * SC, A.is_equal, float(TR), A.mult)
        if t < NSTEP - 1:
            tt(h("BO"), h("NS", 15, 128, 16), h("TB"), A.is_ge)
            ts(h("HAS"), h("XS"), ZC * SC, A.not_equal)
            mms(h("P7", 0, 8), [(h("ONE"), h("BO"))])

    def books2(t):
        ak = AK1 if t % 2 == 0 else AK0
        run("v", lambda: V.tensor_reduce(ap(col(A1)), ap(h("P7", 0, 8)), AX.X, A.add), col(A1), [h("P7", 0, 8)], 64 * CY)
        ts(x8(0), h("TB"), 5.0e5, A.is_lt)
        cp(h("fi", 0, 1), col(A1))
        tt(x8(1), x8(0), h("HAS"), A.subtract)
        ts(h("fi", 0, 1), h("fi", 0, 1), 31, A.bitwise_and)
        cp(h("WX", 0, 128, 16), x8(1))
        ts(col(CA), h("fi", 0, 1), -4096.0, A.mult)
        ts(x8(2), x8(1), -4096.0, A.mult, 8192.0, A.add)
        ts(h("THC"), h("THB"), col(CA), A.add, -4096.0 * 2041 - 2040, A.max)
        scan(h("VB", 256, 384), h("RS1"), h("WX"), 0.0, A.mult, A.add)
        ts(x8(3), h("HAS"), 1.0e6, A.mult)
        tt(h("JN"), h("JS"), h("HAS"), A.subtract)
        tt(h("VB", 0, 128), h("MV"), h("VB", 256, 384), A.mult)
        tt(h("TB"), x8(2), x8(3), A.add)
        tt(col(ak), col(A1), col(K37), A.add)
        tt(h("VB", 384, 512), h("VB", 0, 128), h("Kc"), A.add)

    def new_lists(t):
        ff = h("VB", 256, 384)
        cp(h("si", 0, 64), h("Ue", 0, 64))
        cp(h("si", 64, 128), h("Uo", 0, 64))
        tt(h("tf", 0, 8), h("HX"), h("JZ"), A.add)
        cp(ff, h("F%d" % t))
        ts(h("si"), h("si"), 4095, A.bitwise_and)
        ts(h("oz"), h("tf", 0, 8), 1.0 / 64, A.mult)
        tt(h("sj"), h("si"), ff, A.mult)
        ts(h("sj"), h("sj"), 5, A.logical_shift_right)
        tt(h("si"), h("sj"), ff, A.add)
        ts(h("si"), h("si"), col(AK0 if t % 2 == 0 else AK1), A.add)
        ts(h("sj"), h("si"), 4095, A.bitwise_and)
        cp(ind(h("V", SB, SB + 256), h("oz")), h("sj"))

    cores = T.cores
    start_z(1)
    start_t(1)
    for t in range(NSTEP):
        last = t == NSTEP - 1
        fresh = 1 <= t < NSTEP - 1
        gathers(1)
        if t == 0:
            ts(h("V", 0, 2048), h("vwb"), 4095, A.bitwise_and)
            ts(h("V", 2048, 4096), h("vwb"), 12, A.logical_shift_right)
            refresh_zx("Z0", 0)
            start_z(0)
            start_t(0)
        gathers(0)
        sums(t, 1)
        sums(t, 0)
        if fresh:
            refresh_zx("Z%d" % (t % 2), 1)
        p = (t - 1) % 2
        if t == 0:
            constants()
        else:
            cp(ind(h("V", 0, WIN), h("L%d" % p, 0, 4)), h("F%d" % (t - 1), 0, 64))
            cp(ind(h("V", 0, WIN), h("L%d" % p, 4, 8)), h("rxf", 64 * t - 64, 64 * t))
        keys(t, 1)
        dst = cores[(rank + 1 + t % 3) % len(cores)]
        if not last:
            send(h("rxf", 64 * t, 64 * t + 64), h("F%d" % t, 64, 128), "rf%d" % t, dst)
        dgather(t, 1, 0)
        dgather(t, 1, 1)
        keys(t, 0)
        dgather(t, 0, 0)
        if t == 0:
            constants2()
        extremes(1)
        y_of(t, 1)
        dgather(t, 0, 1)
        books1(t)
        if fresh:
            refresh_zx("Z%d" % (t % 2), 0)
        if not last:
            start_z(1)
        tt(h("fs", 32, 36), h("HX", 0, 4), h("BASE", 0, 4), A.add)
        place(t, 1)
        send(h("rxy", 72 * t, 72 * t + 68), h("msg", 72 * t, 72 * t + 68), "ry%d" % t, dst)
        if fresh:
            relocate_vector()
            relocate_tensor()
            cp(ind(h("Q", 0, WIN), h("L%d" % p)), h("QR"))
        extremes(0)
        y_of(t, 0)
        if not last:
            books2(t)
        place(t, 0)
        yE = h("yE%d" % (t % 2))
        write_half(t, 0, yE)
        if not last:
            start_z(0)
            start_t(1)
            start_t(0)
        new_lists(t)
        if fresh:
            relocate_list()
        if last:
            cp(h("so", 0, 128, 2), h("V", SB, SB + 64))
            cp(h("so", 1, 128, 2), h("V", SB + 64, SB + 128))
            dma("y", "dys", T.ys[:, :], ap(h("so")), None, h("so"))
            zf = "Z%d" % (NSTEP % 2)
            act(h("zo", 0, 128, 2), h(zf, 0, 64), AF.Copy)
            act(h("zo", 1, 128, 2), h(zf, 64, 128), AF.Copy)
            dma("y", "dyz", T.yz[:, :], ap(h("zo")), None, h("zo"))
        src = cores[(rank - 1 - t % 3) % len(cores)]
        landed = len(topo.engines(src, core)[:ENG])
        if not last:
            recv(h("rxf", 64 * t, 64 * t + 64), "rf%d" % t, landed)
        recv(h("rxy", 72 * t, 72 * t + 68), "ry%d" % t, landed)
        rx = h("rxy", 72 * t, 72 * t + 64)
        tt(h("fs", 40, 44), h("rxy", 72 * t + 64, 72 * t + 68), h("BASE", 4, 8), A.add)
        cp(h("L%d" % (t % 2), 4, 8), h("fs", 40, 44))
        write_half(t, 1, rx)
        if t < NSTEP - 2:
            mms(h("P7", 128, 192), [(h("WpR"), yE)])
            mms(h("P7", 192, 256), [(h("WpR"), rx)])
            act(h("QR"), h("P7", 128, 256), AF.Identity, -255.0)
    dma("y", "dyx", T.yx[:, :], ap(h("X", 0, 4096)), None, h("X", 0, 4096))
    schedule()
    for s in sorted(total):
        wait("g", (s, total[s]), {s: total[s]})
